import numpy as np
CORES = [9,10,11,14,17,18,19,22,49,50,51,54]
N = 12
B, TIMES = 128, 3
def setup_inputs(rng):
    return {"x": (rng.standard_normal((N, 128, B), dtype=np.float32) * (0.5 + np.abs(rng.standard_normal((1, 1, B), dtype=np.float32))) / np.float32(np.sqrt(128 * N))), "a": (rng.standard_normal((N, 128, N * 128), dtype=np.float32) / 8)}
def setup_inputs_big(rng):
    d = setup_inputs(rng)
    for k in ("a",): d[k] = (d[k].astype(np.float32) * 1048576.0).astype(d[k].dtype)
    return d
def setup_inputs_small(rng):
    d = setup_inputs(rng)
    for k in ("a",): d[k] = (d[k].astype(np.float32) * (1 / 1048576.0)).astype(d[k].dtype)
    return d
def setup_inputs_apart(rng):
    d = setup_inputs(rng)
    f = (10.0 ** rng.permutation(np.linspace(-1.5, 1.5, N))).astype(np.float32).reshape(N, 1, 1)
    for k in ("a",): d[k] = (d[k].astype(np.float32) * f).astype(d[k].dtype)
    return d
def reference(x, a):
    X, A = x.astype(np.float64), a.astype(np.float64)
    h = X
    for _ in range(TIMES):
        h = np.stack([sum(A[r][:, 128 * j:128 * j + 128].T @ h[j] for j in range(N)) for r in range(N)])
        h = h / np.sqrt((h ** 2).sum(axis=(0, 1)))
        h = h + X
    return {"y": h.astype(np.float32)}

@@ -1,0 +1,339 @@
+from concourse.bass import DstId, RemoteDMATransfer
+from concourse.mybir import AluOpType, AxisListType, ActivationFunctionType
+
+N = 12
+NSIM = 64
+W0 = 128
+W1 = 132
+NTOK = 48
+
+SCRATCH = {
+    "abuf": ("sbuf", [128, N * 128], "float32"),
+    "g0": ("sbuf", [128, N * W0], "float32"),
+    "g1": ("sbuf", [128, N * W1], "float32"),
+    "g2": ("sbuf", [128, N * W1], "float32"),
+    "ones": ("sbuf", [128, 128], "float32"),
+    "ident": ("sbuf", [128, 128], "float32"),
+    "sq1": ("sbuf", [128, 128], "float32"),
+    "u1t": ("sbuf", [128, 128], "float32"),
+    "z2t": ("sbuf", [128, 128], "float32"),
+    "u2t": ("sbuf", [128, 128], "float32"),
+    "jk2": ("sbuf", [128, 128], "float32"),
+    "z3t": ("sbuf", [128, 128], "float32"),
+    "u3t": ("sbuf", [128, 128], "float32"),
+    "jk3": ("sbuf", [128, 128], "float32"),
+    "diag": ("sbuf", [128, 128], "float32"),
+    "yout": ("sbuf", [128, 128], "float32"),
+    "sc": ("sbuf", [128, 64], "float32"),
+    "sa": ("sbuf", [128, 4], "float32"),
+    "sb": ("sbuf", [128, 4], "float32"),
+    "p1": ("psum", [128, 512], "float32"),
+    "ps": ("psum", [128, 512], "float32"),
+    "pt1": ("psum", [128, 512], "float32"),
+    "p2": ("psum", [128, 512], "float32"),
+    "p2t": ("psum", [128, 512], "float32"),
+    "p3t": ("psum", [128, 512], "float32"),
+    "py": ("psum", [128, 512], "float32"),
+}
+SEMAPHORES = (["t%d_%d" % (k, j) for k in range(3) for j in range(N)]
+              + ["k%d" % i for i in range(NTOK)]
+              + ["ldx", "lda0", "lda1", "lda2", "sty", "lsend", "sA", "sB"])
+
+
+def popc(m):
+    return bin(m).count("1")
+
+
+def make_plan(cores, topo):
+    chips = []
+    for c in cores:
+        if topo.chip(c) not in chips:
+            chips.append(topo.chip(c))
+    allc = {X: [c for c in range(NSIM) if topo.chip(c) == X] for X in chips}
+    rk = {X: [c for c in cores if topo.chip(c) == X] for X in chips}
+
+    def can(s, Y):
+        return all(topo.may_write(s, d) for d in allc[Y])
+
+    def masks(s):
+        X = topo.chip(s)
+        on = topo.mask(s, [c for c in allc[X] if c != s][0])
+        off = on
+        for Y in chips:
+            if Y != X:
+                off &= topo.mask(s, allc[Y][0])
+        return on, off, on & ~off
+
+    carrier = {}
+    agents = set()
+    for j, o in enumerate(cores):
+        X = topo.chip(o)
+        for Y in chips:
+            if Y == X:
+                continue
+            if can(o, Y):
+                carrier[(j, Y)] = o
+            else:
+                busy = {}
+                for r in rk[X]:
+                    if can(r, Y):
+                        busy[topo.die(r)] = busy.get(topo.die(r), 0) + 1
+                cand = [c for c in allc[X] if c not in cores and can(c, Y)]
+                h = min(cand, key=lambda c: (busy.get(topo.die(c), 0), -c))
+                carrier[(j, Y)] = h
+                agents.add(h)
+    fwd = {}
+    for Y in chips:
+        load = {c: (0.5 if c in agents else 0.0) for c in allc[Y]}
+        inc_t = [j for j, o in enumerate(cores) if topo.chip(o) != Y]
+        inc_t.sort(key=lambda j: (carrier[(j, Y)] == cores[j], j))
+        for j in inc_t:
+            s = carrier[(j, Y)]
+            late = s != cores[j]
+            f = min(allc[Y], key=lambda c: (load[c], topo.die(c) != topo.die(s), (c in cores) != late, c))
+            load[f] += 1.0
+            fwd[(j, Y)] = f
+
+    est, inc = {}, {}
+    acts = {c: [] for X in chips for c in allc[X]}
+    HOP, ROW = 2.3, 0.08
+
+    def emit(s, j, groups):
+        groups = [(m, ds) for m, ds in groups if ds]
+        for m, ds in groups:
+            for i, d in enumerate(ds):
+                est[(d, j)] = est[(s, j)] + HOP + (i + 1) * 128.0 / popc(m) * ROW
+                inc[(d, j)] = popc(m)
+        acts[s].append((est[(s, j)], j, groups))
+
+    def rot(l, n):
+        n = n % len(l) if l else 0
+        return l[n:] + l[:n]
+
+    nin = {Y: 0 for Y in chips}
+    for j, o in enumerate(cores):
+        X = topo.chip(o)
+        i = rk[X].index(o)
+        on, off, hi = masks(o)
+        est[(o, j)] = 0.0
+        others = [Y for Y in chips if Y != X]
+        hand = []
+        for Y in others:
+            if carrier[(j, Y)] != o and carrier[(j, Y)] not in hand:
+                hand.append(carrier[(j, Y)])
+        out = rot([fwd[(j, Y)] for Y in others if carrier[(j, Y)] == o], i)
+        emit(o, j, [(off, hand + out), (hi, rot([c for c in rk[X] if c != o], i))])
+        for h in hand:
+            emit(h, j, [(masks(h)[1], [fwd[(j, Y)] for Y in others if carrier[(j, Y)] == h])])
+    for j, o in enumerate(cores):
+        for Y in chips:
+            if Y != topo.chip(o):
+                f = fwd[(j, Y)]
+                emit(f, j, [(masks(f)[0], rot([c for c in rk[Y] if c != f], nin[Y]))])
+                nin[Y] += 1
+    for c in acts:
+        acts[c].sort(key=lambda a: (a[0], popc(a[2][0][0]), a[1]))
+
+    stB = {c: [] for c in cores}
+    for X in chips:
+        pairs = [d for Y in chips if Y != X for d in rk[Y]]
+        pairs.sort(key=lambda d: sum(1 for s in rk[X] if topo.may_write(s, d)))
+        for d in pairs:
+            s = min([s for s in rk[X] if topo.may_write(s, d)], key=lambda s: len(stB[s]))
+            stB[s].append(d)
+    return {"chips": chips, "rk": rk, "acts": acts, "inc": inc, "est": est, "stB": stB, "masks": masks}
+
+
+def rank_program(g, core, T, topo):
+    plan = make_plan(T.cores, topo)
+    acts, inc, est = plan["acts"], plan["inc"], plan["est"]
+    if core not in acts or not acts[core]:
+        return
+    S = T.sem
+    rank = T.rank_of(core)
+    gbuf = [T.g0, T.g1, T.g2]
+    wid = [W0, W1, W1]
+    nloc = [0]
+
+    def msg(k, j):
+        return gbuf[k][:, j * wid[k]:(j + 1) * wid[k]]
+
+    def tile(k, j):
+        return gbuf[k][:, j * wid[k]:j * wid[k] + 128]
+
+    def fused(groups, sem, src, dst_of):
+        trs = []
+        for m, ds in groups:
+            ids = []
+            for d in ds:
+                a = topo.addr(d)
+                ids.append(DstId(rid=a[0], pnc=a[1]))
+            trs.append(RemoteDMATransfer(dst_ids=ids, dma_engine_mask=m, remote_sem=sem, srcs=[src],
+                                         dsts=[dst_of(d) for d in ds], alu_op=0))
+            nloc[0] += popc(m)
+        g.remote_dma_fused(trs, local_sem=S.lsend)
+
+    if rank is None:
+        for k in range(3):
+            for _, j, groups in acts[core]:
+                g.wait_ge(S["t%d_%d" % (k, j)], inc[(core, j)])
+                fused(groups, S["t%d_%d" % (k, j)], msg(k, j), lambda d: msg(k, j))
+        g.wait_ge(S.lsend, nloc[0])
+        return
+
+    V, P, Ac, Sy = g.vector, g.tensor, g.scalar, g.sync
+    AF, OP = ActivationFunctionType, AluOpType
+    ntok = [0]
+    waited = set()
+    owntok = {}
+
+    def tok(instr):
+        name = "k%d" % ntok[0]
+        ntok[0] += 1
+        instr.then_inc(S[name], 1)
+        return name
+
+    def need(q, qn, *toks):
+        for t in toks:
+            if (qn, t) not in waited:
+                waited.add((qn, t))
+                q.wait_ge(S[t], 1)
+
+    def needsem(q, qn, name, val):
+        if (qn, name) not in waited:
+            waited.add((qn, name))
+            q.wait_ge(S[name], val)
+
+    def needtile(q, qn, k, j):
+        if j != rank:
+            needsem(q, qn, "t%d_%d" % (k, j), inc[(core, j)])
+        elif k == 0:
+            needsem(q, qn, "ldx", 16)
+        else:
+            need(q, qn, *owntok[k])
+
+    def sc(i):
+        return T.sc[:, 4 * i:4 * i + 1]
+
+    def A(j):
+        return T.abuf[:, j * 128:(j + 1) * 128]
+
+    def g_round(k):
+        for _, j, groups in acts[core]:
+            needtile(g, "g", k, j)
+            fused(groups, S["t%d_%d" % (k, j)], msg(k, j), lambda d: msg(k, j))
+
+    order = sorted(range(N), key=lambda j: -1.0 if j == rank else est[(core, j)])
+
+    Sy.dma_start(msg(0, rank), T.x[:]).then_inc(S.ldx, 16)
+    blocks = []
+    for j in order:
+        if j // 4 not in blocks:
+            blocks.append(j // 4)
+    for i, q in enumerate(blocks):
+        (Ac if i % 2 == 0 else Sy).dma_start(T.abuf[:, q * 512:(q + 1) * 512],
+                                             T.a[:, q * 512:(q + 1) * 512]).then_inc(S["lda%d" % q], 16)
+    t_ones = tok(V.memset(T.ones[:], 1.0))
+    t_pad1 = tok(V.memset(T.g1[:, rank * W1 + 129:rank * W1 + 132], 0.0))
+    t_pad2 = tok(V.memset(T.g2[:, rank * W1 + 129:rank * W1 + 132], 0.0))
+    need(g, "g", t_ones)
+    t_id = tok(g.affine_select(T.ident[:], T.ones[:], [[-1, 128]], OP.is_equal, 0.0, 0, 1))
+
+    g_round(0)
+
+    mm = None
+    for i, j in enumerate(order):
+        needsem(P, "p", "lda%d" % (j // 4), 16)
+        needtile(P, "p", 0, j)
+        mm = P.matmul(T.p1[:, 0:128], A(j), tile(0, j), i == 0, i == N - 1)
+    tW = tok(mm)
+    need(Ac, "a", tW)
+    tSq = tok(Ac.activation(T.sq1[:], T.p1[:, 0:128], AF.Square))
+    need(P, "p", tSq, t_ones)
+    tS = tok(P.matmul(T.ps[:, 0:1], T.sq1[:], T.ones[:, 0:1], True, True))
+    need(V, "v", tSq)
+    tU1 = tok(V.tensor_copy(tile(1, rank), T.p1[:, 0:128]))
+    need(V, "v", tS)
+    tSc = tok(V.tensor_copy(T.g1[:, rank * W1 + 128:rank * W1 + 129], T.ps[:, 0:1]))
+    owntok[1] = [tU1, tSc, t_pad1]
+    g_round(1)
+    need(P, "p", tU1, t_id)
+    tT1 = tok(P.matmul(T.pt1[:, 0:128], tile(1, rank), T.ident[:], True, True))
+    P.matmul(T.p2[:, 0:128], T.ident[:], tile(1, rank), True, False)
+    P.matmul(T.py[:, 0:128], T.ident[:], tile(0, rank), True, False)
+    need(Ac, "a", tT1)
+    tU1T = tok(Ac.activation(T.u1t[:], T.pt1[:, 0:128], AF.Copy))
+
+    def pass_t(k, pt, zt, base):
+        m = None
+        for i, j in enumerate(order):
+            needtile(P, "p", k, j)
+            m = P.matmul(pt[:, 0:128], tile(k, j), A(j), i == 0, i == N - 1)
+        tw = tok(m)
+        for j in order:
+            needtile(V, "v", k, j)
+        tr = tok(V.tensor_reduce(sc(base), gbuf[k][:, 128:N * W1:W1], AxisListType.X, OP.add))
+        need(Ac, "a", tr)
+        tn = tok(Ac.activation(sc(base + 1), sc(base), AF.Sqrt))
+        need(V, "v", tn)
+        td = tok(V.reciprocal(sc(base + 2), sc(base + 1)))
+        need(V, "v", td, tw)
+        return tok(V.tensor_scalar(zt[:], pt[:, 0:128], sc(base + 2), None, OP.mult))
+
+    tZ = pass_t(1, T.p2t, T.z2t, 0)
+    need(P, "p", tZ)
+    tP2 = tok(P.matmul(T.p2[:, 0:128], T.z2t[:], T.ident[:], False, True))
+    need(V, "v", tZ, tU1T)
+    tU2T = tok(V.tensor_tensor(T.u2t[:], T.z2t[:], T.u1t[:], OP.add))
+    need(Ac, "a", tU2T)
+    tS2 = tok(Ac.activation(T.jk2[:], T.u2t[:], AF.Square, accum_out=T.g2[:, rank * W1 + 128:rank * W1 + 129]))
+    need(V, "v", tP2)
+    tU2 = tok(V.tensor_copy(tile(2, rank), T.p2[:, 0:128]))
+    owntok[2] = [tU2, tS2, t_pad2]
+    g_round(2)
+
+    tZ = pass_t(2, T.p3t, T.z3t, 3)
+    need(V, "v", tZ)
+    tU3T = tok(V.tensor_tensor(T.u3t[:], T.z3t[:], T.u1t[:], OP.add))
+    need(Ac, "a", tU3T)
+    tS3 = tok(Ac.activation(T.jk3[:], T.u3t[:], AF.Square, accum_out=sc(6)))
+
+    chips, rk, stB = plan["chips"], plan["rk"], plan["stB"]
+    X = topo.chip(core)
+    on, off, hi = plan["masks"](core)
+    peers = [c for c in rk[X] if c != core]
+
+    def dstA(d):
+        i = [c for c in rk[X] if c != d].index(core)
+        return T.sa[:, i:i + 1]
+
+    def dstB(d):
+        i = [Y for Y in chips if Y != topo.chip(d)].index(X)
+        return T.sb[:, i:i + 1]
+
+    need(g, "g", tS3)
+    fused([(on, peers)], S.sA, sc(6), dstA)
+    V.wait_ge(S.sA, sum(popc(plan["masks"](p)[0]) for p in peers))
+    tC = tok(V.tensor_scalar(sc(7), T.sa[:, 0:1], T.sa[:, 1:2], T.sa[:, 2:3], OP.add, OP.add))
+    need(V, "v", tC, tS3)
+    tCh = tok(V.tensor_tensor(sc(8), sc(7), sc(6), OP.add))
+    if stB[core]:
+        need(g, "g", tCh)
+        fused([(off, stB[core])], S.sB, sc(8), dstB)
+    V.wait_ge(S.sB, sum(popc(plan["masks"](s)[1]) for s in T.cores if core in stB[s]))
+    need(V, "v", tCh)
+    tTot = tok(V.tensor_scalar(sc(9), sc(8), T.sb[:, 0:1], T.sb[:, 1:2], OP.add, OP.add))
+    need(Ac, "a", tTot)
+    tN3 = tok(Ac.activation(sc(10), sc(9), AF.Sqrt))
+    need(V, "v", tN3)
+    tD3 = tok(V.reciprocal(sc(11), sc(10)))
+    need(V, "v", tD3, t_id)
+    tDg = tok(V.tensor_scalar(T.diag[:], T.ident[:], sc(11), None, OP.mult))
+    need(P, "p", tDg, tU3T)
+    tY = tok(P.matmul(T.py[:, 0:128], T.u3t[:], T.diag[:], False, True))
+    need(V, "v", tY)
+    tYo = tok(V.tensor_copy(T.yout[:], T.py[:, 0:128]))
+    need(Sy, "s", tYo)
+    Sy.dma_start(T.y[:], T.yout[:]).then_inc(S.sty, 16)
+    Sy.wait_ge(S.sty, 16)
+    g.wait_ge(S.lsend, nloc[0])

@@ -5,7 +5,7 @@ N = 12
 NSIM = 64
 W0 = 128
 W1 = 132
-NTOK = 48
+NTOK = 72
 
 SCRATCH = {
     "abuf": ("sbuf", [128, N * 128], "float32"),
@@ -15,7 +15,6 @@ SCRATCH = {
     "ones": ("sbuf", [128, 128], "float32"),
     "ident": ("sbuf", [128, 128], "float32"),
     "sq1": ("sbuf", [128, 128], "float32"),
-    "u1t": ("sbuf", [128, 128], "float32"),
     "z2t": ("sbuf", [128, 128], "float32"),
     "u2t": ("sbuf", [128, 128], "float32"),
     "jk2": ("sbuf", [128, 128], "float32"),
@@ -24,8 +23,8 @@ SCRATCH = {
     "jk3": ("sbuf", [128, 128], "float32"),
     "diag": ("sbuf", [128, 128], "float32"),
     "yout": ("sbuf", [128, 128], "float32"),
-    "sc": ("sbuf", [128, 64], "float32"),
-    "sa": ("sbuf", [128, 4], "float32"),
+    "sc": ("sbuf", [128, 256], "float32"),
+    "sa": ("sbuf", [128, 16], "float32"),
     "sb": ("sbuf", [128, 4], "float32"),
     "p1": ("psum", [128, 512], "float32"),
     "ps": ("psum", [128, 512], "float32"),
@@ -37,7 +36,7 @@ SCRATCH = {
 }
 SEMAPHORES = (["t%d_%d" % (k, j) for k in range(3) for j in range(N)]
               + ["k%d" % i for i in range(NTOK)]
-              + ["ldx", "lda0", "lda1", "lda2", "sty", "lsend", "sA", "sB"])
+              + ["ldx", "lda0", "lda1", "lda2", "sty", "lsend", "sA", "sB", "sid"])
 
 
 def popc(m):
@@ -134,6 +133,12 @@ def make_plan(cores, topo):
     for c in acts:
         acts[c].sort(key=lambda a: (a[0], popc(a[2][0][0]), a[1]))
 
+    idto = {}
+    for X in chips:
+        idle = [c for c in allc[X] if c not in cores and acts[c]]
+        for h, r in zip(idle, rk[X]):
+            idto[h] = r
+
     stB = {c: [] for c in cores}
     for X in chips:
         pairs = [d for Y in chips if Y != X for d in rk[Y]]
@@ -141,7 +146,7 @@ def make_plan(cores, topo):
         for d in pairs:
             s = min([s for s in rk[X] if topo.may_write(s, d)], key=lambda s: len(stB[s]))
             stB[s].append(d)
-    return {"chips": chips, "rk": rk, "acts": acts, "inc": inc, "est": est, "stB": stB, "masks": masks}
+    return {"chips": chips, "rk": rk, "acts": acts, "inc": inc, "est": est, "stB": stB, "masks": masks, "idto": idto}
 
 
 def rank_program(g, core, T, topo):
@@ -154,12 +159,18 @@ def rank_program(g, core, T, topo):
     gbuf = [T.g0, T.g1, T.g2]
     wid = [W0, W1, W1]
     nloc = [0]
+    V, P, Ac, Sy = g.vector, g.tensor, g.scalar, g.sync
+    AF, OP = ActivationFunctionType, AluOpType
+    on, off, hi = plan["masks"](core)
 
     def msg(k, j):
         return gbuf[k][:, j * wid[k]:(j + 1) * wid[k]]
 
     def tile(k, j):
         return gbuf[k][:, j * wid[k]:j * wid[k] + 128]
+
+    def scol(k, j):
+        return gbuf[k][:, j * W1 + 128:j * W1 + 129]
 
     def fused(groups, sem, src, dst_of):
         trs = []
@@ -173,7 +184,16 @@ def rank_program(g, core, T, topo):
             nloc[0] += popc(m)
         g.remote_dma_fused(trs, local_sem=S.lsend)
 
+    def make_ident():
+        V.memset(T.ones[:], 1.0).then_inc(S.k0, 1)
+        g.wait_ge(S.k0, 1)
+        return g.affine_select(T.ident[:], T.ones[:], [[-1, 128]], OP.is_equal, 0.0, 0, 1)
+
     if rank is None:
+        if core in plan["idto"]:
+            make_ident().then_inc(S.k1, 1)
+            g.wait_ge(S.k1, 1)
+            fused([(on, [plan["idto"][core]])], S.sid, T.ident[:], lambda d: T.ident[:])
         for k in range(3):
             for _, j, groups in acts[core]:
                 g.wait_ge(S["t%d_%d" % (k, j)], inc[(core, j)])
@@ -181,9 +201,8 @@ def rank_program(g, core, T, topo):
         g.wait_ge(S.lsend, nloc[0])
         return
 
-    V, P, Ac, Sy = g.vector, g.tensor, g.scalar, g.sync
-    AF, OP = ActivationFunctionType, AluOpType
-    ntok = [0]
+    ntok = [2]
+    nsc = [0]
     waited = set()
     owntok = {}
 
@@ -212,8 +231,9 @@ def rank_program(g, core, T, topo):
         else:
             need(q, qn, *owntok[k])
 
-    def sc(i):
-        return T.sc[:, 4 * i:4 * i + 1]
+    def sc():
+        nsc[0] += 1
+        return T.sc[:, 4 * nsc[0] - 4:4 * nsc[0] - 3]
 
     def A(j):
         return T.abuf[:, j * 128:(j + 1) * 128]
@@ -224,6 +244,7 @@ def rank_program(g, core, T, topo):
             fused(groups, S["t%d_%d" % (k, j)], msg(k, j), lambda d: msg(k, j))
 
     order = sorted(range(N), key=lambda j: -1.0 if j == rank else est[(core, j)])
+    foreign = [j for j, o in enumerate(T.cores) if topo.chip(o) != topo.chip(core)]
 
     Sy.dma_start(msg(0, rank), T.x[:]).then_inc(S.ldx, 16)
     blocks = []
@@ -233,11 +254,20 @@ def rank_program(g, core, T, topo):
     for i, q in enumerate(blocks):
         (Ac if i % 2 == 0 else Sy).dma_start(T.abuf[:, q * 512:(q + 1) * 512],
                                              T.a[:, q * 512:(q + 1) * 512]).then_inc(S["lda%d" % q], 16)
-    t_ones = tok(V.memset(T.ones[:], 1.0))
+    idsrc = [h for h in plan["idto"] if plan["idto"][h] == core]
+    if idsrc:
+        t_ones = tok(V.memset(T.ones[:, 0:1], 1.0))
+
+        def need_id(q, qn):
+            needsem(q, qn, "sid", popc(plan["masks"](idsrc[0])[0]))
+    else:
+        t_ones = "k0"
+        make_ident().then_inc(S.k1, 1)
+
+        def need_id(q, qn):
+            need(q, qn, "k1")
     t_pad1 = tok(V.memset(T.g1[:, rank * W1 + 129:rank * W1 + 132], 0.0))
     t_pad2 = tok(V.memset(T.g2[:, rank * W1 + 129:rank * W1 + 132], 0.0))
-    need(g, "g", t_ones)
-    t_id = tok(g.affine_select(T.ident[:], T.ones[:], [[-1, 128]], OP.is_equal, 0.0, 0, 1))
 
     g_round(0)
 
@@ -254,81 +284,119 @@ def rank_program(g, core, T, topo):
     need(V, "v", tSq)
     tU1 = tok(V.tensor_copy(tile(1, rank), T.p1[:, 0:128]))
     need(V, "v", tS)
-    tSc = tok(V.tensor_copy(T.g1[:, rank * W1 + 128:rank * W1 + 129], T.ps[:, 0:1]))
+    tSc = tok(V.tensor_copy(scol(1, rank), T.ps[:, 0:1]))
     owntok[1] = [tU1, tSc, t_pad1]
     g_round(1)
-    need(P, "p", tU1, t_id)
+    need(P, "p", tU1)
+    need_id(P, "p")
     tT1 = tok(P.matmul(T.pt1[:, 0:128], tile(1, rank), T.ident[:], True, True))
     P.matmul(T.p2[:, 0:128], T.ident[:], tile(1, rank), True, False)
     P.matmul(T.py[:, 0:128], T.ident[:], tile(0, rank), True, False)
-    need(Ac, "a", tT1)
-    tU1T = tok(Ac.activation(T.u1t[:], T.pt1[:, 0:128], AF.Copy))
+    u1t = T.pt1[:, 0:128]
 
-    def pass_t(k, pt, zt, base):
+    def runs(js):
+        r = []
+        for j in js:
+            if r and r[-1][1] == j:
+                r[-1][1] = j + 1
+            else:
+                r.append([j, j + 1])
+        return r
+
+    def sums(k, js):
+        cs, ts = [], []
+        for a0, b0 in runs(js):
+            c = sc()
+            cs.append(c)
+            ts.append(tok(V.tensor_reduce(c, gbuf[k][:, a0 * W1 + 128:(b0 - 1) * W1 + 129:W1], AxisListType.X, OP.add)))
+        return cs, ts
+
+    def pass_t(k, pt, zt, late):
         m = None
         for i, j in enumerate(order):
             needtile(P, "p", k, j)
             m = P.matmul(pt[:, 0:128], tile(k, j), A(j), i == 0, i == N - 1)
         tw = tok(m)
         for j in order:
-            needtile(V, "v", k, j)
-        tr = tok(V.tensor_reduce(sc(base), gbuf[k][:, 128:N * W1:W1], AxisListType.X, OP.add))
-        need(Ac, "a", tr)
-        tn = tok(Ac.activation(sc(base + 1), sc(base), AF.Sqrt))
-        need(V, "v", tn)
-        td = tok(V.reciprocal(sc(base + 2), sc(base + 1)))
-        need(V, "v", td, tw)
-        return tok(V.tensor_scalar(zt[:], pt[:, 0:128], sc(base + 2), None, OP.mult))
+            if j not in late:
+                needtile(V, "v", k, j)
+        cs, ts = sums(k, [j for j in range(N) if j not in late])
+        ra, ia, isa, rat, rq, iq = sc(), sc(), sc(), sc(), sc(), sc()
+        need(Ac, "a", ts[0])
+        t = tok(Ac.activation(ra, cs[0], AF.Sqrt))
+        need(V, "v", t)
+        tia = tok(V.reciprocal(ia, ra))
+        need(V, "v", tia)
+        if not late:
+            need(V, "v", tw)
+            return tok(V.tensor_scalar(zt[:], pt[:, 0:128], ia, None, OP.mult))
+        need(V, "v", tok(V.tensor_tensor(isa, ia, ia, OP.mult)))
+        for j in order:
+            if j in late:
+                needtile(V, "v", k, j)
+        cs, ts = sums(k, late)
+        need(V, "v", *ts)
+        if len(cs) == 1:
+            t = tok(V.tensor_scalar(rat, cs[0], isa, None, OP.mult))
+        else:
+            t = tok(V.tensor_scalar(rat, cs[0], cs[1], isa, OP.add, OP.mult))
+        need(Ac, "a", t)
+        t = tok(Ac.activation(rq, rat, AF.Sqrt, bias=1.0))
+        need(V, "v", t)
+        t = tok(V.reciprocal(iq, rq))
+        need(V, "v", t, tw)
+        return tok(V.tensor_scalar(zt[:], pt[:, 0:128], iq, ia, OP.mult, OP.mult))
 
-    tZ = pass_t(1, T.p2t, T.z2t, 0)
+    tZ = pass_t(1, T.p2t, T.z2t, foreign)
     need(P, "p", tZ)
     tP2 = tok(P.matmul(T.p2[:, 0:128], T.z2t[:], T.ident[:], False, True))
-    need(V, "v", tZ, tU1T)
-    tU2T = tok(V.tensor_tensor(T.u2t[:], T.z2t[:], T.u1t[:], OP.add))
+    need(V, "v", tZ, tT1)
+    tU2T = tok(V.tensor_tensor(T.u2t[:], T.z2t[:], u1t, OP.add))
     need(Ac, "a", tU2T)
-    tS2 = tok(Ac.activation(T.jk2[:], T.u2t[:], AF.Square, accum_out=T.g2[:, rank * W1 + 128:rank * W1 + 129]))
+    tS2 = tok(Ac.activation(T.jk2[:], T.u2t[:], AF.Square, accum_out=scol(2, rank)))
     need(V, "v", tP2)
     tU2 = tok(V.tensor_copy(tile(2, rank), T.p2[:, 0:128]))
     owntok[2] = [tU2, tS2, t_pad2]
     g_round(2)
 
-    tZ = pass_t(2, T.p3t, T.z3t, 3)
+    tZ = pass_t(2, T.p3t, T.z3t, [])
     need(V, "v", tZ)
-    tU3T = tok(V.tensor_tensor(T.u3t[:], T.z3t[:], T.u1t[:], OP.add))
+    tU3T = tok(V.tensor_tensor(T.u3t[:], T.z3t[:], u1t, OP.add))
     need(Ac, "a", tU3T)
-    tS3 = tok(Ac.activation(T.jk3[:], T.u3t[:], AF.Square, accum_out=sc(6)))
-
+    ch, tt, n3, d3 = sc(), sc(), sc(), sc()
     chips, rk, stB = plan["chips"], plan["rk"], plan["stB"]
     X = topo.chip(core)
-    on, off, hi = plan["masks"](core)
     peers = [c for c in rk[X] if c != core]
+    npe = len(peers)
+    s3 = T.sa[:, 4 * npe:4 * npe + 1]
+    tS3 = tok(Ac.activation(T.jk3[:], T.u3t[:], AF.Square, accum_out=s3))
 
     def dstA(d):
         i = [c for c in rk[X] if c != d].index(core)
-        return T.sa[:, i:i + 1]
+        return T.sa[:, 4 * i:4 * i + 1]
 
     def dstB(d):
         i = [Y for Y in chips if Y != topo.chip(d)].index(X)
         return T.sb[:, i:i + 1]
 
     need(g, "g", tS3)
-    fused([(on, peers)], S.sA, sc(6), dstA)
+    fused([(on, peers)], S.sA, s3, dstA)
     V.wait_ge(S.sA, sum(popc(plan["masks"](p)[0]) for p in peers))
-    tC = tok(V.tensor_scalar(sc(7), T.sa[:, 0:1], T.sa[:, 1:2], T.sa[:, 2:3], OP.add, OP.add))
-    need(V, "v", tC, tS3)
-    tCh = tok(V.tensor_tensor(sc(8), sc(7), sc(6), OP.add))
+    need(V, "v", tS3)
+    tCh = tok(V.tensor_reduce(ch, T.sa[:, 0:4 * npe + 1:4], AxisListType.X, OP.add))
     if stB[core]:
         need(g, "g", tCh)
-        fused([(off, stB[core])], S.sB, sc(8), dstB)
+        fused([(off, stB[core])], S.sB, ch, dstB)
     V.wait_ge(S.sB, sum(popc(plan["masks"](s)[1]) for s in T.cores if core in stB[s]))
     need(V, "v", tCh)
-    tTot = tok(V.tensor_scalar(sc(9), sc(8), T.sb[:, 0:1], T.sb[:, 1:2], OP.add, OP.add))
+    tTot = tok(V.tensor_scalar(tt, ch, T.sb[:, 0:1], T.sb[:, 1:2], OP.add, OP.add))
     need(Ac, "a", tTot)
-    tN3 = tok(Ac.activation(sc(10), sc(9), AF.Sqrt))
+    tN3 = tok(Ac.activation(n3, tt, AF.Sqrt))
     need(V, "v", tN3)
-    tD3 = tok(V.reciprocal(sc(11), sc(10)))
-    need(V, "v", tD3, t_id)
-    tDg = tok(V.tensor_scalar(T.diag[:], T.ident[:], sc(11), None, OP.mult))
+    tD3 = tok(V.reciprocal(d3, n3))
+    need(V, "v", tD3)
+    need_id(V, "v")
+    tDg = tok(V.tensor_scalar(T.diag[:], T.ident[:], d3, None, OP.mult))
     need(P, "p", tDg, tU3T)
     tY = tok(P.matmul(T.py[:, 0:128], T.u3t[:], T.diag[:], False, True))
     need(V, "v", tY)

from concourse.bass import DstId, RemoteDMATransfer
from concourse.mybir import AluOpType, AxisListType, ActivationFunctionType

N = 12
NSIM = 64
W0 = 128
W1 = 132
NTOK = 72

SCRATCH = {
    "abuf": ("sbuf", [128, N * 128], "float32"),
    "g0": ("sbuf", [128, N * W0], "float32"),
    "g1": ("sbuf", [128, N * W1], "float32"),
    "g2": ("sbuf", [128, N * W1], "float32"),
    "ones": ("sbuf", [128, 128], "float32"),
    "ident": ("sbuf", [128, 128], "float32"),
    "sq1": ("sbuf", [128, 128], "float32"),
    "z2t": ("sbuf", [128, 128], "float32"),
    "u2t": ("sbuf", [128, 128], "float32"),
    "jk2": ("sbuf", [128, 128], "float32"),
    "z3t": ("sbuf", [128, 128], "float32"),
    "u3t": ("sbuf", [128, 128], "float32"),
    "jk3": ("sbuf", [128, 128], "float32"),
    "diag": ("sbuf", [128, 128], "float32"),
    "yout": ("sbuf", [128, 128], "float32"),
    "sc": ("sbuf", [128, 256], "float32"),
    "sa": ("sbuf", [128, 16], "float32"),
    "sb": ("sbuf", [128, 4], "float32"),
    "p1": ("psum", [128, 512], "float32"),
    "ps": ("psum", [128, 512], "float32"),
    "pt1": ("psum", [128, 512], "float32"),
    "p2": ("psum", [128, 512], "float32"),
    "p2t": ("psum", [128, 512], "float32"),
    "p3t": ("psum", [128, 512], "float32"),
    "py": ("psum", [128, 512], "float32"),
}
SEMAPHORES = (["t%d_%d" % (k, j) for k in range(3) for j in range(N)]
              + ["k%d" % i for i in range(NTOK)]
              + ["ldx", "lda0", "lda1", "lda2", "sty", "lsend", "sA", "sB", "sid"])


def popc(m):
    return bin(m).count("1")


def make_plan(cores, topo):
    chips = []
    for c in cores:
        if topo.chip(c) not in chips:
            chips.append(topo.chip(c))
    allc = {X: [c for c in range(NSIM) if topo.chip(c) == X] for X in chips}
    rk = {X: [c for c in cores if topo.chip(c) == X] for X in chips}

    def can(s, Y):
        return all(topo.may_write(s, d) for d in allc[Y])

    def masks(s):
        X = topo.chip(s)
        on = topo.mask(s, [c for c in allc[X] if c != s][0])
        off = on
        for Y in chips:
            if Y != X:
                off &= topo.mask(s, allc[Y][0])
        return on, off, on & ~off

    carrier = {}
    agents = set()
    for j, o in enumerate(cores):
        X = topo.chip(o)
        for Y in chips:
            if Y == X:
                continue
            if can(o, Y):
                carrier[(j, Y)] = o
            else:
                busy = {}
                for r in rk[X]:
                    if can(r, Y):
                        busy[topo.die(r)] = busy.get(topo.die(r), 0) + 1
                cand = [c for c in allc[X] if c not in cores and can(c, Y)]
                h = min(cand, key=lambda c: (busy.get(topo.die(c), 0), -c))
                carrier[(j, Y)] = h
                agents.add(h)
    fwd = {}
    for Y in chips:
        load = {c: (0.5 if c in agents else 0.0) for c in allc[Y]}
        inc_t = [j for j, o in enumerate(cores) if topo.chip(o) != Y]
        inc_t.sort(key=lambda j: (carrier[(j, Y)] == cores[j], j))
        for j in inc_t:
            s = carrier[(j, Y)]
            late = s != cores[j]
            f = min(allc[Y], key=lambda c: (load[c], topo.die(c) != topo.die(s), (c in cores) != late, c))
            load[f] += 1.0
            fwd[(j, Y)] = f

    est, inc = {}, {}
    acts = {c: [] for X in chips for c in allc[X]}
    HOP, ROW = 2.3, 0.08

    def emit(s, j, groups):
        groups = [(m, ds) for m, ds in groups if ds]
        for m, ds in groups:
            for i, d in enumerate(ds):
                est[(d, j)] = est[(s, j)] + HOP + (i + 1) * 128.0 / popc(m) * ROW
                inc[(d, j)] = popc(m)
        acts[s].append((est[(s, j)], j, groups))

    def rot(l, n):
        n = n % len(l) if l else 0
        return l[n:] + l[:n]

    nin = {Y: 0 for Y in chips}
    for j, o in enumerate(cores):
        X = topo.chip(o)
        i = rk[X].index(o)
        on, off, hi = masks(o)
        est[(o, j)] = 0.0
        others = [Y for Y in chips if Y != X]
        hand = []
        for Y in others:
            if carrier[(j, Y)] != o and carrier[(j, Y)] not in hand:
                hand.append(carrier[(j, Y)])
        out = rot([fwd[(j, Y)] for Y in others if carrier[(j, Y)] == o], i)
        emit(o, j, [(off, hand + out), (hi, rot([c for c in rk[X] if c != o], i))])
        for h in hand:
            emit(h, j, [(masks(h)[1], [fwd[(j, Y)] for Y in others if carrier[(j, Y)] == h])])
    for j, o in enumerate(cores):
        for Y in chips:
            if Y != topo.chip(o):
                f = fwd[(j, Y)]
                emit(f, j, [(masks(f)[0], rot([c for c in rk[Y] if c != f], nin[Y]))])
                nin[Y] += 1
    for c in acts:
        acts[c].sort(key=lambda a: (a[0], popc(a[2][0][0]), a[1]))

    idto = {}
    for X in chips:
        idle = [c for c in allc[X] if c not in cores and acts[c]]
        for h, r in zip(idle, rk[X]):
            idto[h] = r

    stB = {c: [] for c in cores}
    for X in chips:
        pairs = [d for Y in chips if Y != X for d in rk[Y]]
        pairs.sort(key=lambda d: sum(1 for s in rk[X] if topo.may_write(s, d)))
        for d in pairs:
            s = min([s for s in rk[X] if topo.may_write(s, d)], key=lambda s: len(stB[s]))
            stB[s].append(d)
    return {"chips": chips, "rk": rk, "acts": acts, "inc": inc, "est": est, "stB": stB, "masks": masks, "idto": idto}


def rank_program(g, core, T, topo):
    plan = make_plan(T.cores, topo)
    acts, inc, est = plan["acts"], plan["inc"], plan["est"]
    if core not in acts or not acts[core]:
        return
    S = T.sem
    rank = T.rank_of(core)
    gbuf = [T.g0, T.g1, T.g2]
    wid = [W0, W1, W1]
    nloc = [0]
    V, P, Ac, Sy = g.vector, g.tensor, g.scalar, g.sync
    AF, OP = ActivationFunctionType, AluOpType
    on, off, hi = plan["masks"](core)

    def msg(k, j):
        return gbuf[k][:, j * wid[k]:(j + 1) * wid[k]]

    def tile(k, j):
        return gbuf[k][:, j * wid[k]:j * wid[k] + 128]

    def scol(k, j):
        return gbuf[k][:, j * W1 + 128:j * W1 + 129]

    def fused(groups, sem, src, dst_of):
        trs = []
        for m, ds in groups:
            ids = []
            for d in ds:
                a = topo.addr(d)
                ids.append(DstId(rid=a[0], pnc=a[1]))
            trs.append(RemoteDMATransfer(dst_ids=ids, dma_engine_mask=m, remote_sem=sem, srcs=[src],
                                         dsts=[dst_of(d) for d in ds], alu_op=0))
            nloc[0] += popc(m)
        g.remote_dma_fused(trs, local_sem=S.lsend)

    def make_ident():
        V.memset(T.ones[:], 1.0).then_inc(S.k0, 1)
        g.wait_ge(S.k0, 1)
        return g.affine_select(T.ident[:], T.ones[:], [[-1, 128]], OP.is_equal, 0.0, 0, 1)

    if rank is None:
        if core in plan["idto"]:
            make_ident().then_inc(S.k1, 1)
            g.wait_ge(S.k1, 1)
            fused([(on, [plan["idto"][core]])], S.sid, T.ident[:], lambda d: T.ident[:])
        for k in range(3):
            for _, j, groups in acts[core]:
                g.wait_ge(S["t%d_%d" % (k, j)], inc[(core, j)])
                fused(groups, S["t%d_%d" % (k, j)], msg(k, j), lambda d: msg(k, j))
        g.wait_ge(S.lsend, nloc[0])
        return

    ntok = [2]
    nsc = [0]
    waited = set()
    owntok = {}

    def tok(instr):
        name = "k%d" % ntok[0]
        ntok[0] += 1
        instr.then_inc(S[name], 1)
        return name

    def need(q, qn, *toks):
        for t in toks:
            if (qn, t) not in waited:
                waited.add((qn, t))
                q.wait_ge(S[t], 1)

    def needsem(q, qn, name, val):
        if (qn, name) not in waited:
            waited.add((qn, name))
            q.wait_ge(S[name], val)

    def needtile(q, qn, k, j):
        if j != rank:
            needsem(q, qn, "t%d_%d" % (k, j), inc[(core, j)])
        elif k == 0:
            needsem(q, qn, "ldx", 16)
        else:
            need(q, qn, *owntok[k])

    def sc():
        nsc[0] += 1
        return T.sc[:, 4 * nsc[0] - 4:4 * nsc[0] - 3]

    def A(j):
        return T.abuf[:, j * 128:(j + 1) * 128]

    def g_round(k):
        for _, j, groups in acts[core]:
            needtile(g, "g", k, j)
            fused(groups, S["t%d_%d" % (k, j)], msg(k, j), lambda d: msg(k, j))

    order = sorted(range(N), key=lambda j: -1.0 if j == rank else est[(core, j)])
    foreign = [j for j, o in enumerate(T.cores) if topo.chip(o) != topo.chip(core)]

    Sy.dma_start(msg(0, rank), T.x[:]).then_inc(S.ldx, 16)
    blocks = []
    for j in order:
        if j // 4 not in blocks:
            blocks.append(j // 4)
    for i, q in enumerate(blocks):
        (Ac if i % 2 == 0 else Sy).dma_start(T.abuf[:, q * 512:(q + 1) * 512],
                                             T.a[:, q * 512:(q + 1) * 512]).then_inc(S["lda%d" % q], 16)
    idsrc = [h for h in plan["idto"] if plan["idto"][h] == core]
    if idsrc:
        t_ones = tok(V.memset(T.ones[:, 0:1], 1.0))

        def need_id(q, qn):
            needsem(q, qn, "sid", popc(plan["masks"](idsrc[0])[0]))
    else:
        t_ones = "k0"
        make_ident().then_inc(S.k1, 1)

        def need_id(q, qn):
            need(q, qn, "k1")
    t_pad1 = tok(V.memset(T.g1[:, rank * W1 + 129:rank * W1 + 132], 0.0))
    t_pad2 = tok(V.memset(T.g2[:, rank * W1 + 129:rank * W1 + 132], 0.0))

    g_round(0)

    mm = None
    for i, j in enumerate(order):
        needsem(P, "p", "lda%d" % (j // 4), 16)
        needtile(P, "p", 0, j)
        mm = P.matmul(T.p1[:, 0:128], A(j), tile(0, j), i == 0, i == N - 1)
    tW = tok(mm)
    need(Ac, "a", tW)
    tSq = tok(Ac.activation(T.sq1[:], T.p1[:, 0:128], AF.Square))
    need(P, "p", tSq, t_ones)
    tS = tok(P.matmul(T.ps[:, 0:1], T.sq1[:], T.ones[:, 0:1], True, True))
    need(V, "v", tSq)
    tU1 = tok(V.tensor_copy(tile(1, rank), T.p1[:, 0:128]))
    need(V, "v", tS)
    tSc = tok(V.tensor_copy(scol(1, rank), T.ps[:, 0:1]))
    owntok[1] = [tU1, tSc, t_pad1]
    g_round(1)
    need(P, "p", tU1)
    need_id(P, "p")
    tT1 = tok(P.matmul(T.pt1[:, 0:128], tile(1, rank), T.ident[:], True, True))
    P.matmul(T.p2[:, 0:128], T.ident[:], tile(1, rank), True, False)
    P.matmul(T.py[:, 0:128], T.ident[:], tile(0, rank), True, False)
    u1t = T.pt1[:, 0:128]

    def runs(js):
        r = []
        for j in js:
            if r and r[-1][1] == j:
                r[-1][1] = j + 1
            else:
                r.append([j, j + 1])
        return r

    def sums(k, js):
        cs, ts = [], []
        for a0, b0 in runs(js):
            c = sc()
            cs.append(c)
            ts.append(tok(V.tensor_reduce(c, gbuf[k][:, a0 * W1 + 128:(b0 - 1) * W1 + 129:W1], AxisListType.X, OP.add)))
        return cs, ts

    def pass_t(k, pt, zt, late):
        m = None
        for i, j in enumerate(order):
            needtile(P, "p", k, j)
            m = P.matmul(pt[:, 0:128], tile(k, j), A(j), i == 0, i == N - 1)
        tw = tok(m)
        for j in order:
            if j not in late:
                needtile(V, "v", k, j)
        cs, ts = sums(k, [j for j in range(N) if j not in late])
        ra, ia, isa, rat, rq, iq = sc(), sc(), sc(), sc(), sc(), sc()
        need(Ac, "a", ts[0])
        t = tok(Ac.activation(ra, cs[0], AF.Sqrt))
        need(V, "v", t)
        tia = tok(V.reciprocal(ia, ra))
        need(V, "v", tia)
        if not late:
            need(V, "v", tw)
            return tok(V.tensor_scalar(zt[:], pt[:, 0:128], ia, None, OP.mult))
        need(V, "v", tok(V.tensor_tensor(isa, ia, ia, OP.mult)))
        for j in order:
            if j in late:
                needtile(V, "v", k, j)
        cs, ts = sums(k, late)
        need(V, "v", *ts)
        if len(cs) == 1:
            t = tok(V.tensor_scalar(rat, cs[0], isa, None, OP.mult))
        else:
            t = tok(V.tensor_scalar(rat, cs[0], cs[1], isa, OP.add, OP.mult))
        need(Ac, "a", t)
        t = tok(Ac.activation(rq, rat, AF.Sqrt, bias=1.0))
        need(V, "v", t)
        t = tok(V.reciprocal(iq, rq))
        need(V, "v", t, tw)
        return tok(V.tensor_scalar(zt[:], pt[:, 0:128], iq, ia, OP.mult, OP.mult))

    tZ = pass_t(1, T.p2t, T.z2t, foreign)
    need(P, "p", tZ)
    tP2 = tok(P.matmul(T.p2[:, 0:128], T.z2t[:], T.ident[:], False, True))
    need(V, "v", tZ, tT1)
    tU2T = tok(V.tensor_tensor(T.u2t[:], T.z2t[:], u1t, OP.add))
    need(Ac, "a", tU2T)
    tS2 = tok(Ac.activation(T.jk2[:], T.u2t[:], AF.Square, accum_out=scol(2, rank)))
    need(V, "v", tP2)
    tU2 = tok(V.tensor_copy(tile(2, rank), T.p2[:, 0:128]))
    owntok[2] = [tU2, tS2, t_pad2]
    g_round(2)

    tZ = pass_t(2, T.p3t, T.z3t, [])
    need(V, "v", tZ)
    tU3T = tok(V.tensor_tensor(T.u3t[:], T.z3t[:], u1t, OP.add))
    need(Ac, "a", tU3T)
    ch, tt, n3, d3 = sc(), sc(), sc(), sc()
    chips, rk, stB = plan["chips"], plan["rk"], plan["stB"]
    X = topo.chip(core)
    peers = [c for c in rk[X] if c != core]
    npe = len(peers)
    s3 = T.sa[:, 4 * npe:4 * npe + 1]
    tS3 = tok(Ac.activation(T.jk3[:], T.u3t[:], AF.Square, accum_out=s3))

    def dstA(d):
        i = [c for c in rk[X] if c != d].index(core)
        return T.sa[:, 4 * i:4 * i + 1]

    def dstB(d):
        i = [Y for Y in chips if Y != topo.chip(d)].index(X)
        return T.sb[:, i:i + 1]

    need(g, "g", tS3)
    fused([(on, peers)], S.sA, s3, dstA)
    V.wait_ge(S.sA, sum(popc(plan["masks"](p)[0]) for p in peers))
    need(V, "v", tS3)
    tCh = tok(V.tensor_reduce(ch, T.sa[:, 0:4 * npe + 1:4], AxisListType.X, OP.add))
    if stB[core]:
        need(g, "g", tCh)
        fused([(off, stB[core])], S.sB, ch, dstB)
    V.wait_ge(S.sB, sum(popc(plan["masks"](s)[1]) for s in T.cores if core in stB[s]))
    need(V, "v", tCh)
    tTot = tok(V.tensor_scalar(tt, ch, T.sb[:, 0:1], T.sb[:, 1:2], OP.add, OP.add))
    need(Ac, "a", tTot)
    tN3 = tok(Ac.activation(n3, tt, AF.Sqrt))
    need(V, "v", tN3)
    tD3 = tok(V.reciprocal(d3, n3))
    need(V, "v", tD3)
    need_id(V, "v")
    tDg = tok(V.tensor_scalar(T.diag[:], T.ident[:], d3, None, OP.mult))
    need(P, "p", tDg, tU3T)
    tY = tok(P.matmul(T.py[:, 0:128], T.u3t[:], T.diag[:], False, True))
    need(V, "v", tY)
    tYo = tok(V.tensor_copy(T.yout[:], T.py[:, 0:128]))
    need(Sy, "s", tYo)
    Sy.dma_start(T.y[:], T.yout[:]).then_inc(S.sty, 16)
    Sy.wait_ge(S.sty, 16)
    g.wait_ge(S.lsend, nloc[0])
